import numpy as np
import ml_dtypes


def mxq(x, axis, fmt="e4m3"):
    dtype, down = {"e4m3": (ml_dtypes.float8_e4m3fn, 7), "e5m2": (ml_dtypes.float8_e5m2, 14)}[fmt]
    v = np.moveaxis(np.asarray(x, np.float32).astype(ml_dtypes.bfloat16).astype(np.float64), axis, -1)
    blocks = v.reshape(v.shape[:-1] + (-1, 32))
    amax = np.abs(blocks).max(-1, keepdims=True)
    byte = np.maximum(np.where(amax > 0, np.frexp(amax)[1] - 1 + 127, 0) - down, 1)
    scale = np.exp2(byte - 127.0)
    codes = (blocks / scale).astype(np.float32).astype(dtype).astype(np.float64)
    return np.moveaxis((codes * scale).reshape(v.shape), -1, axis)


WIDE = False


def mx_kscale(k):
    if not WIDE:
        return np.ones(k)
    levels = np.array([10, -10, 5, -5, 0])
    if k % 512:
        return np.exp2(np.random.permutation(np.resize(levels, k // 32))).repeat(32)
    a = np.empty((k // 512, 16))
    for p in range(k // 512):
        a[p, :8] = np.random.permutation(np.resize(levels, 8))
        for g in range(8):
            far = levels[np.abs(levels - a[p, g]) >= 10]
            a[p, g + 8] = far[np.random.randint(len(far))]
    return np.exp2(a.ravel()).repeat(32)


def f64(x):
    return np.asarray(x).astype(np.float64)


def striped(idx):
    return np.tile(idx.reshape(-1, 16).T, (8, 1)).astype(np.uint16)


def unstriped(offs):
    return offs[:16].T.reshape(-1).astype(np.int64)


E2M1 = np.array([0.0, 0.5, 1.0, 1.5, 2.0, 3.0, 4.0, 6.0, -0.0, -0.5, -1.0, -1.5, -2.0, -3.0, -4.0, -6.0])


def pack_weight(w, fmt):
    k, n = w.shape
    w = f64(np.asarray(w, np.float32).astype(ml_dtypes.bfloat16)).reshape(k // 32, 32, n)
    amax = np.abs(w).max(1)
    if fmt == "e4m3":
        byte = np.frexp(amax)[1] - 1 + 127 - 7
    else:
        mant, ex = np.frexp(amax / 6.0)
        byte = np.where(mant > 0.5, ex, ex - 1) + 127
    byte = np.clip(np.where(amax > 0, byte, 1), 1, 254)
    scaled = (w * np.exp2(127.0 - byte)[:, None, :]).reshape(k, n).astype(np.float32)
    by_word = np.ascontiguousarray(scaled.reshape(k // 512, 128, 4, n).transpose(0, 1, 3, 2))
    if fmt == "e4m3":
        words = by_word.astype(ml_dtypes.float8_e4m3fn).view(np.uint8)
    else:
        c = by_word.astype(ml_dtypes.float4_e2m1fn).view(np.uint8) & 0xF
        words = (c[..., 0::2] | (c[..., 1::2] << 4)).reshape(k // 512, 128, 2 * n)
    return np.ascontiguousarray(words), np.ascontiguousarray(byte.astype(np.uint8).reshape(k // 512, 16, n))


def unpack_weight(words, scales, fmt):
    g, _, n = scales.shape
    words = np.ascontiguousarray(words).reshape(g, 128, n, -1)
    if fmt == "e4m3":
        vals = words.view(ml_dtypes.float8_e4m3fn).astype(np.float64)
    else:
        nib = np.empty((g, 128, n, 4), np.uint8)
        nib[..., 0::2] = words & 0xF
        nib[..., 1::2] = words >> 4
        vals = E2M1[nib]
    vals = vals * np.repeat(np.exp2(scales.astype(np.float64) - 127.0), 8, axis=1)[..., None]
    return vals.transpose(0, 1, 3, 2).reshape(g * 512, n)


def gelu(v):
    return 0.5 * v * (1.0 + np.tanh(np.sqrt(2.0 / np.pi) * (v + 0.044715 * v**3)))


K, KU, KL, T, S, H, T2, P = 1536, 1024, 512, 2048, 512, 1024, 1024, 512

def setup_inputs():
    n = np.random.standard_normal
    s = mx_kscale(K)[:, None]
    u = mx_kscale(H)[:, None]
    d = {}
    d["tab_words"], d["tab_scales"] = pack_weight(n((K, T)) * s, "e4m3")
    d["offs"] = striped(np.random.permutation(T)[:S])
    d["w4_words"], d["w4_scales"] = pack_weight(n((KU, H)) / K**0.5 / s[:KU] * u.T, "e2m1")
    d["w1"] = (n((KL, H)) / K**0.5 / s[KU:] * u.T).astype(np.float32)
    d["frq"] = (np.random.uniform(0.38, 0.55, H) / u[:, 0]).astype(np.float32)
    d["gain"] = (-np.random.uniform(3.2, 5.2, H) * u[:, 0]).astype(np.float32)
    d["page0"] = (0.8 * n((H, T2)) * u).astype(np.float32)
    d["wgs"] = np.exp(0.3 * n((128, S))).astype(np.float32)
    d["offs2"] = striped(np.random.permutation(T2)[:S])
    d["offs3"] = striped(np.random.permutation(T2)[:P])
    d["low"] = (0.5 * n(H) * u[:, 0]).astype(np.float32)
    d["vec"] = (1.5 * n(H) / H**0.5 / u[:, 0]**2).astype(np.float32)
    d["slot"] = np.random.uniform(0.6, 2.0, T2).astype(np.float32)
    return d

def reference(tab_words, tab_scales, offs, w4_words, w4_scales, w1, frq, gain, page0, wgs, offs2, offs3, low, vec, slot):
    v = unpack_weight(tab_words, tab_scales, "e4m3")[:, unstriped(offs)]
    w4 = unpack_weight(w4_words, w4_scales, "e2m1")
    w1q = mxq(f64(w1), 0, "e4m3")
    y = w4.T @ v[:KU] + w1q.T @ v[KU:]
    h = y + f64(gain)[:, None] * np.sin(f64(frq)[:, None] * y)
    page = f64(page0).copy()
    page[:, unstriped(offs2)] = np.tile(f64(wgs), (H // 128, 1)) * h
    x = np.maximum(page[:, unstriped(offs3)], f64(low)[:, None]) * f64(vec)[:, None]
    e = mxq(page, 0, "e4m3").T @ mxq(x, 0, "e4m3")
    return 1.0 / (np.square(e) + f64(slot)[:, None])

@@ -1,0 +1,347 @@
+import math
+from contextlib import ExitStack
+
+import concourse.mybir as mybir
+
+F32 = mybir.dt.float32
+BF16 = mybir.dt.bfloat16
+I32 = mybir.dt.int32
+U32 = mybir.dt.uint32
+U16 = mybir.dt.uint16
+U8 = mybir.dt.uint8
+FP8X4 = mybir.dt.float8_e4m3fn_x4
+FP4X4 = mybir.dt.float4_e2m1fn_x4
+ALU = mybir.AluOpType
+ACT = mybir.ActivationFunctionType
+
+P = 128
+PACK = 4
+T = 2048
+S = 512
+H = 1024
+T2 = 1024
+PICK = 512
+GROUP = P * PACK
+GROUPS = H // GROUP
+SLICES = GROUPS * PACK
+
+VECTOR_SQUARED = 2
+FLOPS = 2 * 1536 * H * S + 2 * H * T2 * PICK
+
+
+def tile_list_launch_field_advisor_kernel(
+    tc, tab_words, tab_scales, offs, w4_words, w4_scales, w1, frq, gain, page0, wgs, offs2, offs3, low, vec, slot, out
+):
+    nc = tc.nc
+    with ExitStack() as ctx:
+        lists = ctx.enter_context(tc.tile_pool(name="lists", bufs=1))
+        keep = ctx.enter_context(tc.tile_pool(name="keep", bufs=1))
+        psum = ctx.enter_context(tc.psum_pool(name="psum", bufs=1))
+
+        list1 = lists.tile([P, S // 16], U16, name="list1")
+        list2 = lists.tile([P, S // 16], U16, name="list2")
+        list3 = lists.tile([P, PICK // 16], U16, name="list3")
+
+        tab = [keep.tile([P, T], U32, name="tab%d" % a) for a in range(3)]
+        tab_sc = keep.tile([P, 2 * T], U8, name="tab_sc")
+        w4_sc_raw = keep.tile([P, 2, H], U8, name="w4_sc_raw")
+        w1_raw = [keep.tile([P, PACK, GROUP], F32, name="w1_raw%d" % b, tag="wide%d" % b, align_bytes=64) for b in range(GROUPS)]
+        w4_raw = [keep.tile([P, 2, 2 * GROUP], U8, name="w4_raw%d" % b) for b in range(GROUPS)]
+        page = [keep.tile([P, T2], F32, name="page%d" % s) for s in range(SLICES)]
+        wg_first = keep.tile([P, S], F32, name="wg_first")
+        wg_rest = keep.tile([P, PACK - 1, S], F32, name="wg_rest")
+        frq_t = keep.tile([P, GROUPS, PACK], F32, name="frq_t")
+        gain_t = keep.tile([P, GROUPS, PACK], F32, name="gain_t")
+        low_t = keep.tile([P, GROUPS, PACK], F32, name="low_t")
+        vec_t = keep.tile([P, GROUPS, PACK], F32, name="vec_t")
+        slot_t = keep.tile([P, T2 // P], F32, name="slot_t")
+
+        def load_tab(a):
+            nc.sync.dma_start(out=tab[a][:].bitcast(I32), in_=tab_words[a].rearrange("p t i -> p (t i)").bitcast(I32))
+
+        def load_w1(b):
+            nc.sync.dma_start(out=w1_raw[b][:], in_=w1[:, b * GROUP:(b + 1) * GROUP].rearrange("(p j) c -> p j c", j=PACK))
+
+        def load_w4(b):
+            nc.sync.dma_start(
+                out=w4_raw[b][:].bitcast(I32),
+                in_=w4_words[:, :, 2 * b * GROUP:2 * (b + 1) * GROUP].rearrange("a p c -> p a c").bitcast(I32),
+            )
+
+        def load_rows(tile, vector):
+            nc.sync.dma_start(out=tile[:], in_=vector.rearrange("(b p t) -> p b t", p=P, t=PACK))
+
+        def load_page(s):
+            b, t = divmod(s, PACK)
+            nc.sync.dma_start(out=page[s][:], in_=page0[b * GROUP:(b + 1) * GROUP, :].rearrange("(p t) m -> p t m", t=PACK)[:, t, :])
+
+        nc.vector.memset(tab_sc[:].bitcast(I32), 0)
+        nc.vector.memset(w4_sc_raw[:].rearrange("p a c -> p (a c)").bitcast(I32), 0)
+
+        def load_tab_scales(q):
+            nc.sync.dma_start(
+                out=tab_sc[32 * q:32 * q + 4, :].rearrange("r (a t) -> r a t", a=2).bitcast(I32),
+                in_=tab_scales[0:2, 4 * q:4 * q + 4, :].rearrange("a r t -> r a t").bitcast(I32),
+            )
+
+        def load_w4_scales(q):
+            nc.sync.dma_start(
+                out=w4_sc_raw[32 * q:32 * q + 4, :, :].bitcast(I32),
+                in_=w4_scales[:, 4 * q:4 * q + 4, :].rearrange("a r c -> r a c").bitcast(I32),
+            )
+
+        def load_last_scales(q):
+            nc.sync.dma_start(
+                out=tab_sc[32 * q + 4:32 * q + 8, 0:T].bitcast(I32),
+                in_=tab_scales[2, 4 * q:4 * q + 4, :].bitcast(I32),
+            )
+
+        nc.sync.dma_start(list1[:], offs)
+        load_rows(frq_t, frq)
+        load_rows(gain_t, gain)
+        load_tab(1)
+        for q in range(4):
+            load_tab_scales(q)
+        load_w1(0)
+        for q in range(4):
+            load_w4_scales(q)
+        load_w4(0)
+        load_tab(0)
+        for q in range(4):
+            load_last_scales(q)
+        load_tab(2)
+        nc.sync.dma_start(list2[:], offs2)
+        load_page(0)
+        wgs_rows = wgs.rearrange("(p t) j -> p t j", t=PACK)
+        for q in (0, 2, 1, 3):
+            nc.sync.dma_start(out=wg_first[32 * q:32 * (q + 1), :], in_=wgs_rows[:, 0, :])
+        for q in (0, 2, 1, 3):
+            nc.sync.dma_start(out=wg_rest[32 * q:32 * (q + 1), :, :], in_=wgs_rows[:, 1:PACK, :])
+        nc.sync.dma_start(list3[:], offs3)
+        load_rows(low_t, low)
+        load_rows(vec_t, vec)
+        load_page(1)
+        load_w1(1)
+        load_w4(1)
+        for s in range(2, SLICES):
+            load_page(s)
+        with nc.allow_non_contiguous_dma(reason="one slot value for each output row"):
+            nc.sync.dma_start(out=slot_t[:], in_=slot.rearrange("(c p) -> p c", p=P))
+
+        half_frq = keep.tile([P, GROUPS, PACK], F32, name="half_frq")
+        gain_m2 = keep.tile([P, GROUPS, PACK], F32, name="gain_m2")
+        shift = keep.tile([P, 1], F32, name="shift")
+        nc.vector.memset(shift[:], 1.0)
+        nc.scalar.activation(out=shift[:], in_=shift[:], func=ACT.Copy, scale=-math.pi / 4)
+        nc.scalar.activation(out=half_frq[:], in_=frq_t[:], func=ACT.Copy, scale=0.5)
+        nc.scalar.activation(out=gain_m2[:], in_=gain_t[:], func=ACT.Copy, scale=-2.0)
+
+        picked = [keep.tile([P, S], U32, name="picked%d" % a, align_bytes=64) for a in range(3)]
+        picked_sc = [keep.tile([P, S], U8, name="picked_sc%d" % w, align_bytes=64) for w in range(2)]
+        nc.vector.tensor_copy(picked[1][:], tab[1][:].indirect(list1[:]))
+        nc.vector.tensor_copy(picked_sc[1][:], tab_sc[:, T:2 * T].indirect(list1[:]))
+
+        w1_codes = [keep.tile([P, GROUP], U32, name="w1_codes%d" % b, align_bytes=64) for b in range(GROUPS)]
+        w1_sc = [keep.tile([P, GROUP], U8, name="w1_sc%d" % b, align_bytes=64) for b in range(GROUPS)]
+        w4_codes = [keep.tile([P, 2, 2 * GROUP], U8, name="w4_codes%d" % b, align_bytes=64) for b in range(GROUPS)]
+        w4_sc = [keep.tile([P, 2, GROUP], U8, name="w4_sc%d" % b, align_bytes=64) for b in range(GROUPS)]
+
+        def prepare_weights(b):
+            w1_bf = keep.tile([P, GROUP * PACK], BF16, name="w1_bf", align_bytes=64)
+            nc.scalar.copy(
+                out=w1_bf[:].rearrange("p (t q j) -> p q j t", t=PACK, j=PACK),
+                in_=w1_raw[b][:].rearrange("p j (q t) -> p q j t", t=PACK),
+            )
+            nc.scalar.copy(
+                out=w4_codes[b][:].bitcast(U16).rearrange("p a (t q) -> p a t q", t=PACK),
+                in_=w4_raw[b][:].bitcast(U16).rearrange("p a (q t) -> p a t q", t=PACK),
+            )
+            nc.vector.quantize_mx(out=w1_codes[b][:].bitcast(FP8X4), scales=w1_sc[b][:], in_=w1_bf[:])
+
+        def deal_w4_scales(b):
+            nc.vector.tensor_copy(
+                out=w4_sc[b][:].rearrange("p a (t q) -> p a t q", t=PACK),
+                in_=w4_sc_raw[:, :, b * GROUP:(b + 1) * GROUP].rearrange("p a (q t) -> p a t q", t=PACK),
+            )
+
+        deal_w4_scales(0)
+        prepare_weights(0)
+        nc.vector.tensor_copy(picked[0][:], tab[0][:].indirect(list1[:]))
+        nc.vector.tensor_copy(picked_sc[0][:], tab_sc[:, 0:T].indirect(list1[:]))
+        half = S // 2
+        for c0 in (0, half):
+            nc.vector.tensor_copy(picked[2][:, c0:c0 + half], tab[2][:].indirect(list1[:, c0 // 16:(c0 + half) // 16]))
+
+        deal_w4_scales(1)
+
+        y = {}
+        wave = {}
+        sq = {}
+
+        def first_product(s, c0, c1, bank):
+            b, t = divmod(s, PACK)
+            acc = psum.tile([P, c1 - c0], F32, name="y%d_%d" % (s, c0), tag="bank%d" % bank)
+            for a in (1, 0):
+                nc.tensor.matmul_mx(
+                    out=acc[:],
+                    lhsT=w4_codes[b][:, a, 2 * P * t:2 * P * (t + 1)].bitcast(FP4X4),
+                    lhsT_scale=w4_sc[b][:, a, P * t:P * (t + 1)],
+                    rhs=picked[a][:, c0:c1].bitcast(FP8X4),
+                    rhs_scale=picked_sc[a][:, c0:c1],
+                    start=(a == 1),
+                    stop=False,
+                )
+            nc.tensor.matmul_mx(
+                out=acc[:],
+                lhsT=w1_codes[b][:, P * t:P * (t + 1)].bitcast(FP8X4),
+                lhsT_scale=w1_sc[b][:, P * t:P * (t + 1)],
+                rhs=picked[2][:, c0:c1].bitcast(FP8X4),
+                rhs_scale=picked_sc[0][4:P, c0:c1],
+                start=False,
+                stop=True,
+            )
+            y[s, c0] = acc
+
+        def sine(s, parts):
+            b, t = divmod(s, PACK)
+            z = wave[s] = keep.tile([P, S], F32, name="wave%d" % s, tag="wave%d" % s)
+            q = keep.tile([P, S], F32, name="sq%d" % s, tag="stage%d" % s)
+            for c0, c1 in parts:
+                nc.scalar.activation(out=z[:, c0:c1], in_=y[s, c0][:], func=ACT.Sin, bias=shift[:], scale=half_frq[:, b, t:t + 1])
+            for c0, c1 in parts:
+                nc.scalar.activation(out=q[:, c0:c1], in_=z[:, c0:c1], func=ACT.Square)
+            for c0, c1 in parts:
+                nc.scalar.activation(
+                    out=z[:, c0:c1], in_=q[:, c0:c1], func=ACT.Identity, bias=gain_t[:, b, t:t + 1], scale=gain_m2[:, b, t:t + 1]
+                )
+
+        halves = ((0, half), (half, S))
+        whole = ((0, S),)
+        first_product(0, 0, half, 0)
+        first_product(0, half, S, SLICES - 1)
+        sine(0, halves)
+        for c0, c1 in halves:
+            nc.vector.tensor_tensor(out=wave[0][:, c0:c1], in0=y[0, c0][:], in1=wave[0][:, c0:c1], op=ALU.add)
+        for s in range(1, PACK):
+            first_product(s, 0, S, s)
+            sine(s, whole)
+        prepare_weights(1)
+        for s in range(PACK, SLICES):
+            first_product(s, 0, S, s)
+            sine(s, whole)
+
+        joined_lanes = (4, 2)
+        x_f32 = [keep.tile([P, joined_lanes[b], PICK], F32, name="x_f32_%d" % b) for b in range(GROUPS)]
+        x_bf = [keep.tile([P, PICK, PACK], BF16, name="x_bf%d" % b, tag="narrow%d" % b, align_bytes=64) for b in range(GROUPS)]
+        x_codes = [keep.tile([P, PICK], U32, name="x_codes%d" % b, align_bytes=64) for b in range(GROUPS)]
+        x_sc = [keep.tile([P, PICK], U8, name="x_sc%d" % b, align_bytes=64) for b in range(GROUPS)]
+        chunk = 2 * P
+        chunks = T2 // chunk
+        page_bf0 = keep.tile([P, T2, PACK], BF16, name="page_bf0", tag="wide0", align_bytes=64)
+        page_bf1 = [keep.tile([P, chunk, PACK], BF16, name="page_bf1_%d" % c, align_bytes=64) for c in range(chunks)]
+        page_codes = [keep.tile([P, T2], U32, name="page_codes%d" % b, align_bytes=64) for b in range(GROUPS)]
+        page_sc = [keep.tile([P, T2], U8, name="page_sc%d" % b, align_bytes=64) for b in range(GROUPS)]
+        joined = [keep.tile([P, joined_lanes[b], T2], F32, name="joined%d" % b) for b in range(GROUPS)]
+
+        def interleave(dst, src, lanes):
+            nc.scalar.copy(
+                out=dst[:, :, 0:lanes].rearrange("p (c i) t -> p c t i", i=4),
+                in_=src.rearrange("p t (c i) -> p c t i", i=4),
+            )
+
+        h = {}
+        fetched = {}
+
+        def add(s, tag=None):
+            h[s] = wave[s] if tag is None else keep.tile([P, S], F32, name="h%d" % s, tag=tag, align_bytes=64)
+            nc.vector.tensor_tensor(out=h[s][:], in0=y[s, 0][:], in1=wave[s][:], op=ALU.add)
+
+        def put(s):
+            b, t = divmod(s, PACK)
+            nc.vector.tensor_tensor(page[s][:].indirect(list2[:]), h[s][:], wg_first[:] if t == 0 else wg_rest[:, t - 1, :], ALU.mult)
+            if t < joined_lanes[b]:
+                nc.sync.dma_start(out=joined[b][:, t, :], in_=page[s][:])
+
+        def fetch(s):
+            fetched[s] = keep.tile([P, PICK], F32, name="fetched%d" % s, tag="stage%d" % ((s + 1) % SLICES))
+            nc.vector.tensor_copy(fetched[s][:], page[s][:].indirect(list3[:]))
+
+        def clamp(s):
+            b, t = divmod(s, PACK)
+            dst = x_f32[b][:, t, :] if t < joined_lanes[b] else x_bf[b][:, :, t]
+            nc.vector.tensor_scalar(dst, fetched[s][:], low_t[:, b, t:t + 1], vec_t[:, b, t:t + 1], ALU.max, ALU.mult)
+
+        def quantize(codes, scales, values):
+            nc.vector.quantize_mx(out=codes.bitcast(FP8X4), scales=scales, in_=values[:].rearrange("p c t -> p (c t)"))
+
+        def quantize_chunk(c):
+            cols = slice(c * chunk, (c + 1) * chunk)
+            quantize(page_codes[1][:, cols], page_sc[1][:, cols], page_bf1[c])
+
+        def copy_lane(t):
+            for c in range(chunks):
+                nc.scalar.copy(out=page_bf1[c][:, :, t], in_=page[PACK + t][:, c * chunk:(c + 1) * chunk])
+
+        scores = []
+
+        def second_product(mt, b):
+            if b == 0:
+                scores.append(psum.tile([P, PICK], F32, name="e%d" % mt, tag="bank%d" % mt))
+            nc.tensor.matmul_mx(
+                out=scores[mt][:],
+                lhsT=page_codes[b][:, P * mt:P * (mt + 1)].bitcast(FP8X4),
+                lhsT_scale=page_sc[b][:, P * mt:P * (mt + 1)],
+                rhs=x_codes[b][:].bitcast(FP8X4),
+                rhs_scale=x_sc[b][:],
+                start=(b == 0),
+                stop=(b == GROUPS - 1),
+            )
+
+        for c0, c1 in halves:
+            nc.vector.tensor_tensor(page[0][:].indirect(list2[:, c0 // 16:c1 // 16]), wave[0][:, c0:c1], wg_first[:, c0:c1], ALU.mult)
+        nc.sync.dma_start(out=joined[0][:, 0, :], in_=page[0][:])
+        for s in range(1, 6):
+            add(s)
+            fetch(s - 1)
+            put(s)
+            clamp(s - 1)
+            if s == PACK:
+                interleave(x_bf[0], x_f32[0][:], PACK)
+                interleave(page_bf0, joined[0][:], PACK)
+        for c in range(chunks):
+            interleave(page_bf1[c], joined[1][:, :, c * chunk:(c + 1) * chunk], 2)
+        quantize(x_codes[0][:], x_sc[0][:], x_bf[0])
+        add(6, "narrow0")
+        fetch(5)
+        put(6)
+        clamp(5)
+        copy_lane(2)
+        interleave(x_bf[1], x_f32[1][:], 2)
+        quantize(page_codes[0][:], page_sc[0][:], page_bf0)
+        add(7, "wide0")
+        fetch(6)
+        put(7)
+        clamp(6)
+        for mt in range(T2 // P):
+            second_product(mt, 0)
+        copy_lane(3)
+        fetch(7)
+        quantize_chunk(0)
+        clamp(7)
+        quantize_chunk(1)
+        quantize(x_codes[1][:], x_sc[1][:], x_bf[1])
+        for c in range(2, chunks):
+            quantize_chunk(c)
+
+        for mt in range(T2 // P):
+            second_product(mt, 1)
+            root = keep.tile([P, PICK], F32, name="root%d" % mt, tag="wave%d" % mt)
+            result = keep.tile([P, PICK], F32, name="result%d" % mt, tag="stage%d" % mt)
+            if mt < VECTOR_SQUARED:
+                nc.vector.tensor_copy(out=result[:], in_=scores[mt][:])
+                nc.vector.tensor_tensor(out=root[:], in0=scores[mt][:], in1=result[:], op=ALU.mult)
+            else:
+                nc.scalar.activation(out=root[:], in_=scores[mt][:], func=ACT.Square)
+            nc.scalar.activation(out=root[:], in_=root[:], func=ACT.Abs_reciprocal_sqrt, bias=slot_t[:, mt:mt + 1])
+            nc.vector.tensor_tensor(out=result[:], in0=root[:], in1=root[:], op=ALU.mult)
+            nc.sync.dma_start(out=out[P * mt:P * (mt + 1), :], in_=result[:])

@@ -25,7 +25,8 @@ GROUP = P * PACK
 GROUPS = H // GROUP
 SLICES = GROUPS * PACK
 
-VECTOR_SQUARED = 2
+VECTOR_SQUARED = (1, 3, 5)
+QUADRANTS = (0, 2, 1, 3)
 FLOPS = 2 * 1536 * H * S + 2 * H * T2 * PICK
 
 
@@ -78,50 +79,35 @@ def tile_list_launch_field_advisor_kernel(
         nc.vector.memset(tab_sc[:].bitcast(I32), 0)
         nc.vector.memset(w4_sc_raw[:].rearrange("p a c -> p (a c)").bitcast(I32), 0)
 
-        def load_tab_scales(q):
-            nc.sync.dma_start(
-                out=tab_sc[32 * q:32 * q + 4, :].rearrange("r (a t) -> r a t", a=2).bitcast(I32),
-                in_=tab_scales[0:2, 4 * q:4 * q + 4, :].rearrange("a r t -> r a t").bitcast(I32),
-            )
-
-        def load_w4_scales(q):
-            nc.sync.dma_start(
-                out=w4_sc_raw[32 * q:32 * q + 4, :, :].bitcast(I32),
-                in_=w4_scales[:, 4 * q:4 * q + 4, :].rearrange("a r c -> r a c").bitcast(I32),
-            )
-
-        def load_last_scales(q):
-            nc.sync.dma_start(
-                out=tab_sc[32 * q + 4:32 * q + 8, 0:T].bitcast(I32),
-                in_=tab_scales[2, 4 * q:4 * q + 4, :].bitcast(I32),
-            )
-
         nc.sync.dma_start(list1[:], offs)
         load_rows(frq_t, frq)
         load_rows(gain_t, gain)
         load_tab(1)
-        for q in range(4):
-            load_tab_scales(q)
+        for q in QUADRANTS:
+            nc.sync.dma_start(out=tab_sc[32 * q:32 * q + 4, T:2 * T].bitcast(I32), in_=tab_scales[1, 4 * q:4 * q + 4, :].bitcast(I32))
         load_w1(0)
-        for q in range(4):
-            load_w4_scales(q)
+        for q in QUADRANTS:
+            nc.sync.dma_start(
+                out=w4_sc_raw[32 * q:32 * q + 4, :, :].bitcast(I32),
+                in_=w4_scales[:, 4 * q:4 * q + 4, :].rearrange("a r c -> r a c").bitcast(I32),
+            )
         load_w4(0)
         load_tab(0)
-        for q in range(4):
-            load_last_scales(q)
-        load_tab(2)
+        for q in QUADRANTS:
+            nc.sync.dma_start(out=tab_sc[32 * q:32 * q + 8, 0:T].bitcast(I32), in_=tab_scales[0:3:2, 4 * q:4 * q + 4, :].bitcast(I32))
         nc.sync.dma_start(list2[:], offs2)
+        load_tab(2)
         load_page(0)
         wgs_rows = wgs.rearrange("(p t) j -> p t j", t=PACK)
-        for q in (0, 2, 1, 3):
+        for q in QUADRANTS:
             nc.sync.dma_start(out=wg_first[32 * q:32 * (q + 1), :], in_=wgs_rows[:, 0, :])
-        for q in (0, 2, 1, 3):
+        for q in QUADRANTS:
             nc.sync.dma_start(out=wg_rest[32 * q:32 * (q + 1), :, :], in_=wgs_rows[:, 1:PACK, :])
+        load_page(1)
         nc.sync.dma_start(list3[:], offs3)
+        load_w1(1)
         load_rows(low_t, low)
         load_rows(vec_t, vec)
-        load_page(1)
-        load_w1(1)
         load_w4(1)
         for s in range(2, SLICES):
             load_page(s)
@@ -171,6 +157,7 @@ def tile_list_launch_field_advisor_kernel(
         half = S // 2
         for c0 in (0, half):
             nc.vector.tensor_copy(picked[2][:, c0:c0 + half], tab[2][:].indirect(list1[:, c0 // 16:(c0 + half) // 16]))
+
 
         deal_w4_scales(1)
 
@@ -222,32 +209,29 @@ def tile_list_launch_field_advisor_kernel(
         sine(0, halves)
         for c0, c1 in halves:
             nc.vector.tensor_tensor(out=wave[0][:, c0:c1], in0=y[0, c0][:], in1=wave[0][:, c0:c1], op=ALU.add)
-        for s in range(1, PACK):
+        for s in range(1, SLICES):
             first_product(s, 0, S, s)
             sine(s, whole)
-        prepare_weights(1)
-        for s in range(PACK, SLICES):
-            first_product(s, 0, S, s)
-            sine(s, whole)
+            if s == 1:
+                prepare_weights(1)
 
-        joined_lanes = (4, 2)
-        x_f32 = [keep.tile([P, joined_lanes[b], PICK], F32, name="x_f32_%d" % b) for b in range(GROUPS)]
-        x_bf = [keep.tile([P, PICK, PACK], BF16, name="x_bf%d" % b, tag="narrow%d" % b, align_bytes=64) for b in range(GROUPS)]
-        x_codes = [keep.tile([P, PICK], U32, name="x_codes%d" % b, align_bytes=64) for b in range(GROUPS)]
-        x_sc = [keep.tile([P, PICK], U8, name="x_sc%d" % b, align_bytes=64) for b in range(GROUPS)]
         chunk = 2 * P
         chunks = T2 // chunk
-        page_bf0 = keep.tile([P, T2, PACK], BF16, name="page_bf0", tag="wide0", align_bytes=64)
+        x_pair = [keep.tile([P, 2, PICK], F32, name="x_pair%d" % i) for i in range(3)]
+        page_pair = [keep.tile([P, 2, T2], F32, name="page_pair%d" % i) for i in range(2)]
+        x_bf0 = [keep.tile([P, PICK // 2, PACK], BF16, name="x_bf0_%d" % i, tag="narrow%d" % i, align_bytes=64) for i in range(2)]
+        x_bf1 = keep.tile([P, PICK, PACK], BF16, name="x_bf1", align_bytes=64)
+        page_bf0 = [keep.tile([P, T2 // 2, PACK], BF16, name="page_bf0_%d" % i, tag="wide%d" % i, align_bytes=64) for i in range(2)]
         page_bf1 = [keep.tile([P, chunk, PACK], BF16, name="page_bf1_%d" % c, align_bytes=64) for c in range(chunks)]
+        x_codes = [keep.tile([P, PICK], U32, name="x_codes%d" % b, align_bytes=64) for b in range(GROUPS)]
+        x_sc = [keep.tile([P, PICK], U8, name="x_sc%d" % b, align_bytes=64) for b in range(GROUPS)]
         page_codes = [keep.tile([P, T2], U32, name="page_codes%d" % b, align_bytes=64) for b in range(GROUPS)]
         page_sc = [keep.tile([P, T2], U8, name="page_sc%d" % b, align_bytes=64) for b in range(GROUPS)]
-        joined = [keep.tile([P, joined_lanes[b], T2], F32, name="joined%d" % b) for b in range(GROUPS)]
 
-        def interleave(dst, src, lanes):
-            nc.scalar.copy(
-                out=dst[:, :, 0:lanes].rearrange("p (c i) t -> p c t i", i=4),
-                in_=src.rearrange("p t (c i) -> p c t i", i=4),
-            )
+        def weave_pair(tiles, pair, t0):
+            width = pair.shape[2] // len(tiles)
+            for n, dst in enumerate(tiles):
+                nc.scalar.copy(out=dst[:, :, t0:t0 + 2], in_=pair[:, :, n * width:(n + 1) * width].rearrange("p t c -> p c t"))
 
         h = {}
         fetched = {}
@@ -259,16 +243,19 @@ def tile_list_launch_field_advisor_kernel(
         def put(s):
             b, t = divmod(s, PACK)
             nc.vector.tensor_tensor(page[s][:].indirect(list2[:]), h[s][:], wg_first[:] if t == 0 else wg_rest[:, t - 1, :], ALU.mult)
-            if t < joined_lanes[b]:
-                nc.sync.dma_start(out=joined[b][:, t, :], in_=page[s][:])
+            if b == 0:
+                nc.sync.dma_start(out=page_pair[t // 2][:, t % 2, :], in_=page[s][:])
 
-        def fetch(s):
-            fetched[s] = keep.tile([P, PICK], F32, name="fetched%d" % s, tag="stage%d" % ((s + 1) % SLICES))
+        def fetch(s, tag=None):
+            if tag is None:
+                fetched[s] = keep.tile([P, PICK], F32, name="fetched%d" % s, tag="stage%d" % ((s + 1) % SLICES))
+            else:
+                fetched[s] = keep.tile([P, PICK], F32, name="fetched%d" % s, tag=tag, align_bytes=64)
             nc.vector.tensor_copy(fetched[s][:], page[s][:].indirect(list3[:]))
 
         def clamp(s):
             b, t = divmod(s, PACK)
-            dst = x_f32[b][:, t, :] if t < joined_lanes[b] else x_bf[b][:, :, t]
+            dst = x_pair[s // 2][:, s % 2, :] if s < 6 else x_bf1[:, :, t]
             nc.vector.tensor_scalar(dst, fetched[s][:], low_t[:, b, t:t + 1], vec_t[:, b, t:t + 1], ALU.max, ALU.mult)
 
         def quantize(codes, scales, values):
@@ -299,29 +286,34 @@ def tile_list_launch_field_advisor_kernel(
 
         for c0, c1 in halves:
             nc.vector.tensor_tensor(page[0][:].indirect(list2[:, c0 // 16:c1 // 16]), wave[0][:, c0:c1], wg_first[:, c0:c1], ALU.mult)
-        nc.sync.dma_start(out=joined[0][:, 0, :], in_=page[0][:])
+        nc.sync.dma_start(out=page_pair[0][:, 0, :], in_=page[0][:])
         for s in range(1, 6):
             add(s)
             fetch(s - 1)
             put(s)
             clamp(s - 1)
-            if s == PACK:
-                interleave(x_bf[0], x_f32[0][:], PACK)
-                interleave(page_bf0, joined[0][:], PACK)
-        for c in range(chunks):
-            interleave(page_bf1[c], joined[1][:, :, c * chunk:(c + 1) * chunk], 2)
-        quantize(x_codes[0][:], x_sc[0][:], x_bf[0])
-        add(6, "narrow0")
-        fetch(5)
-        put(6)
+            if s in (1, 3):
+                weave_pair(page_bf0, page_pair[s // 2], s - 1)
+            if s in (2, 4):
+                weave_pair(x_bf0, x_pair[s // 2 - 1], s - 2)
+            if s >= PACK:
+                copy_lane(s - PACK)
+        for i in range(2):
+            cols = slice(i * PICK // 2, (i + 1) * PICK // 2)
+            quantize(x_codes[0][:, cols], x_sc[0][:, cols], x_bf0[i])
+        fetch(5, "narrow0")
+        add(6, "narrow1")
         clamp(5)
+        put(6)
+        weave_pair([x_bf1], x_pair[2], 0)
         copy_lane(2)
-        interleave(x_bf[1], x_f32[1][:], 2)
-        quantize(page_codes[0][:], page_sc[0][:], page_bf0)
-        add(7, "wide0")
-        fetch(6)
-        put(7)
+        for i in range(2):
+            cols = slice(i * T2 // 2, (i + 1) * T2 // 2)
+            quantize(page_codes[0][:, cols], page_sc[0][:, cols], page_bf0[i])
+        fetch(6, "wide0")
+        add(7, "wide1")
         clamp(6)
+        put(7)
         for mt in range(T2 // P):
             second_product(mt, 0)
         copy_lane(3)
@@ -329,7 +321,7 @@ def tile_list_launch_field_advisor_kernel(
         quantize_chunk(0)
         clamp(7)
         quantize_chunk(1)
-        quantize(x_codes[1][:], x_sc[1][:], x_bf[1])
+        quantize(x_codes[1][:], x_sc[1][:], x_bf1)
         for c in range(2, chunks):
             quantize_chunk(c)
 
@@ -337,7 +329,7 @@ def tile_list_launch_field_advisor_kernel(
             second_product(mt, 1)
             root = keep.tile([P, PICK], F32, name="root%d" % mt, tag="wave%d" % mt)
             result = keep.tile([P, PICK], F32, name="result%d" % mt, tag="stage%d" % mt)
-            if mt < VECTOR_SQUARED:
+            if mt in VECTOR_SQUARED:
                 nc.vector.tensor_copy(out=result[:], in_=scores[mt][:])
                 nc.vector.tensor_tensor(out=root[:], in0=scores[mt][:], in1=result[:], op=ALU.mult)
             else:

@@ -55,7 +55,6 @@ def tile_list_launch_field_advisor_kernel(
         gain_t = keep.tile([P, GROUPS, PACK], F32, name="gain_t")
         low_t = keep.tile([P, GROUPS, PACK], F32, name="low_t")
         vec_t = keep.tile([P, GROUPS, PACK], F32, name="vec_t")
-        slot_t = keep.tile([P, T2 // P], F32, name="slot_t")
 
         def load_tab(a):
             nc.sync.dma_start(out=tab[a][:].bitcast(I32), in_=tab_words[a].rearrange("p t i -> p (t i)").bitcast(I32))
@@ -69,22 +68,22 @@ def tile_list_launch_field_advisor_kernel(
                 in_=w4_words[:, :, 2 * b * GROUP:2 * (b + 1) * GROUP].rearrange("a p c -> p a c").bitcast(I32),
             )
 
-        def load_rows(tile, vector):
-            nc.sync.dma_start(out=tile[:], in_=vector.rearrange("(b p t) -> p b t", p=P, t=PACK))
+        def load_rows(queue, tile, vector):
+            queue.dma_start(out=tile[:], in_=vector.rearrange("(b p t) -> p b t", p=P, t=PACK))
 
         def load_page(s):
             b, t = divmod(s, PACK)
             nc.sync.dma_start(out=page[s][:], in_=page0[b * GROUP:(b + 1) * GROUP, :].rearrange("(p t) m -> p t m", t=PACK)[:, t, :])
 
         nc.vector.memset(tab_sc[:].bitcast(I32), 0)
-        nc.vector.memset(w4_sc_raw[:].rearrange("p a c -> p (a c)").bitcast(I32), 0)
+        nc.gpsimd.memset(w4_sc_raw[:].rearrange("p a c -> p (a c)").bitcast(I32), 0)
 
         nc.sync.dma_start(list1[:], offs)
-        load_rows(frq_t, frq)
-        load_rows(gain_t, gain)
+        load_rows(nc.scalar, frq_t, frq)
+        load_rows(nc.scalar, gain_t, gain)
         load_tab(1)
         for q in QUADRANTS:
-            nc.sync.dma_start(out=tab_sc[32 * q:32 * q + 4, T:2 * T].bitcast(I32), in_=tab_scales[1, 4 * q:4 * q + 4, :].bitcast(I32))
+            nc.scalar.dma_start(out=tab_sc[32 * q:32 * q + 4, T:2 * T].bitcast(I32), in_=tab_scales[1, 4 * q:4 * q + 4, :].bitcast(I32))
         load_w1(0)
         for q in QUADRANTS:
             nc.sync.dma_start(
@@ -106,13 +105,11 @@ def tile_list_launch_field_advisor_kernel(
         load_page(1)
         nc.sync.dma_start(list3[:], offs3)
         load_w1(1)
-        load_rows(low_t, low)
-        load_rows(vec_t, vec)
+        load_rows(nc.sync, low_t, low)
+        load_rows(nc.sync, vec_t, vec)
         load_w4(1)
         for s in range(2, SLICES):
             load_page(s)
-        with nc.allow_non_contiguous_dma(reason="one slot value for each output row"):
-            nc.sync.dma_start(out=slot_t[:], in_=slot.rearrange("(c p) -> p c", p=P))
 
         half_frq = keep.tile([P, GROUPS, PACK], F32, name="half_frq")
         gain_m2 = keep.tile([P, GROUPS, PACK], F32, name="gain_m2")
@@ -217,7 +214,7 @@ def tile_list_launch_field_advisor_kernel(
 
         chunk = 2 * P
         chunks = T2 // chunk
-        x_pair = [keep.tile([P, 2, PICK], F32, name="x_pair%d" % i) for i in range(3)]
+        x_pair = [keep.tile([P, 2, PICK], F32, name="x_pair%d" % i, tag="x_pair%d" % i) for i in range(3)]
         page_pair = [keep.tile([P, 2, T2], F32, name="page_pair%d" % i) for i in range(2)]
         x_bf0 = [keep.tile([P, PICK // 2, PACK], BF16, name="x_bf0_%d" % i, tag="narrow%d" % i, align_bytes=64) for i in range(2)]
         x_bf1 = keep.tile([P, PICK, PACK], BF16, name="x_bf1", align_bytes=64)
@@ -298,6 +295,9 @@ def tile_list_launch_field_advisor_kernel(
                 weave_pair(x_bf0, x_pair[s // 2 - 1], s - 2)
             if s >= PACK:
                 copy_lane(s - PACK)
+        slot_t = keep.tile([P, T2 // P], F32, name="slot_t", tag="x_pair0")
+        with nc.allow_non_contiguous_dma(reason="one slot value for each output row"):
+            nc.sync.dma_start(out=slot_t[:], in_=slot.rearrange("(c p) -> p c", p=P))
         for i in range(2):
             cols = slice(i * PICK // 2, (i + 1) * PICK // 2)
             quantize(x_codes[0][:, cols], x_sc[0][:, cols], x_bf0[i])

@@ -16,6 +16,7 @@ ACT = mybir.ActivationFunctionType
 
 P = 128
 PACK = 4
+K = 1536
 T = 2048
 S = 512
 H = 1024
@@ -24,10 +25,11 @@ PICK = 512
 GROUP = P * PACK
 GROUPS = H // GROUP
 SLICES = GROUPS * PACK
+FIRST_DIRECT = SLICES - 2
 
 VECTOR_SQUARED = (1, 3, 5)
 QUADRANTS = (0, 2, 1, 3)
-FLOPS = 2 * 1536 * H * S + 2 * H * T2 * PICK
+FLOPS = 2 * K * H * S + 2 * H * T2 * PICK
 
 
 def tile_list_launch_field_advisor_kernel(
@@ -43,7 +45,7 @@ def tile_list_launch_field_advisor_kernel(
         list2 = lists.tile([P, S // 16], U16, name="list2")
         list3 = lists.tile([P, PICK // 16], U16, name="list3")
 
-        tab = [keep.tile([P, T], U32, name="tab%d" % a) for a in range(3)]
+        tab = [keep.tile([P, T], U32, name="tab%d" % a) for a in range(K // GROUP)]
         tab_sc = keep.tile([P, 2 * T], U8, name="tab_sc")
         w4_sc_raw = keep.tile([P, 2, H], U8, name="w4_sc_raw")
         w1_raw = [keep.tile([P, PACK, GROUP], F32, name="w1_raw%d" % b, tag="wide%d" % b, align_bytes=64) for b in range(GROUPS)]
@@ -119,7 +121,7 @@ def tile_list_launch_field_advisor_kernel(
         nc.scalar.activation(out=half_frq[:], in_=frq_t[:], func=ACT.Copy, scale=0.5)
         nc.scalar.activation(out=gain_m2[:], in_=gain_t[:], func=ACT.Copy, scale=-2.0)
 
-        picked = [keep.tile([P, S], U32, name="picked%d" % a, align_bytes=64) for a in range(3)]
+        picked = [keep.tile([P, S], U32, name="picked%d" % a, align_bytes=64) for a in range(K // GROUP)]
         picked_sc = [keep.tile([P, S], U8, name="picked_sc%d" % w, align_bytes=64) for w in range(2)]
         nc.vector.tensor_copy(picked[1][:], tab[1][:].indirect(list1[:]))
         nc.vector.tensor_copy(picked_sc[1][:], tab_sc[:, T:2 * T].indirect(list1[:]))
@@ -154,13 +156,10 @@ def tile_list_launch_field_advisor_kernel(
         half = S // 2
         for c0 in (0, half):
             nc.vector.tensor_copy(picked[2][:, c0:c0 + half], tab[2][:].indirect(list1[:, c0 // 16:(c0 + half) // 16]))
-
-
         deal_w4_scales(1)
 
         y = {}
         wave = {}
-        sq = {}
 
         def first_product(s, c0, c1, bank):
             b, t = divmod(s, PACK)
@@ -189,15 +188,16 @@ def tile_list_launch_field_advisor_kernel(
         def sine(s, parts):
             b, t = divmod(s, PACK)
             z = wave[s] = keep.tile([P, S], F32, name="wave%d" % s, tag="wave%d" % s)
-            q = keep.tile([P, S], F32, name="sq%d" % s, tag="stage%d" % s)
+            squared = keep.tile([P, S], F32, name="sq%d" % s, tag="stage%d" % s)
             for c0, c1 in parts:
                 nc.scalar.activation(out=z[:, c0:c1], in_=y[s, c0][:], func=ACT.Sin, bias=shift[:], scale=half_frq[:, b, t:t + 1])
             for c0, c1 in parts:
-                nc.scalar.activation(out=q[:, c0:c1], in_=z[:, c0:c1], func=ACT.Square)
+                nc.scalar.activation(out=squared[:, c0:c1], in_=z[:, c0:c1], func=ACT.Square)
             for c0, c1 in parts:
                 nc.scalar.activation(
-                    out=z[:, c0:c1], in_=q[:, c0:c1], func=ACT.Identity, bias=gain_t[:, b, t:t + 1], scale=gain_m2[:, b, t:t + 1]
+                    out=z[:, c0:c1], in_=squared[:, c0:c1], func=ACT.Identity, bias=gain_t[:, b, t:t + 1], scale=gain_m2[:, b, t:t + 1]
                 )
+            return squared
 
         halves = ((0, half), (half, S))
         whole = ((0, S),)
@@ -208,13 +208,16 @@ def tile_list_launch_field_advisor_kernel(
             nc.vector.tensor_tensor(out=wave[0][:, c0:c1], in0=y[0, c0][:], in1=wave[0][:, c0:c1], op=ALU.add)
         for s in range(1, SLICES):
             first_product(s, 0, S, s)
-            sine(s, whole)
+            last_squared = sine(s, whole)
             if s == 1:
                 prepare_weights(1)
 
+        warm = keep.tile([P, 1], F32, name="warm")
+        nc.scalar.activation(out=warm[:], in_=last_squared[:, 0:1], func=ACT.Abs_reciprocal_sqrt, bias=shift[:], scale=-1.0)
+
         chunk = 2 * P
         chunks = T2 // chunk
-        x_pair = [keep.tile([P, 2, PICK], F32, name="x_pair%d" % i, tag="x_pair%d" % i) for i in range(3)]
+        x_pair = [keep.tile([P, 2, PICK], F32, name="x_pair%d" % i, tag="x_pair%d" % i) for i in range(FIRST_DIRECT // 2)]
         page_pair = [keep.tile([P, 2, T2], F32, name="page_pair%d" % i) for i in range(2)]
         x_bf0 = [keep.tile([P, PICK // 2, PACK], BF16, name="x_bf0_%d" % i, tag="narrow%d" % i, align_bytes=64) for i in range(2)]
         x_bf1 = keep.tile([P, PICK, PACK], BF16, name="x_bf1", align_bytes=64)
@@ -252,7 +255,7 @@ def tile_list_launch_field_advisor_kernel(
 
         def clamp(s):
             b, t = divmod(s, PACK)
-            dst = x_pair[s // 2][:, s % 2, :] if s < 6 else x_bf1[:, :, t]
+            dst = x_pair[s // 2][:, s % 2, :] if s < FIRST_DIRECT else x_bf1[:, :, t]
             nc.vector.tensor_scalar(dst, fetched[s][:], low_t[:, b, t:t + 1], vec_t[:, b, t:t + 1], ALU.max, ALU.mult)
 
         def quantize(codes, scales, values):
@@ -284,14 +287,14 @@ def tile_list_launch_field_advisor_kernel(
         for c0, c1 in halves:
             nc.vector.tensor_tensor(page[0][:].indirect(list2[:, c0 // 16:c1 // 16]), wave[0][:, c0:c1], wg_first[:, c0:c1], ALU.mult)
         nc.sync.dma_start(out=page_pair[0][:, 0, :], in_=page[0][:])
-        for s in range(1, 6):
+        for s in range(1, FIRST_DIRECT):
             add(s)
             fetch(s - 1)
             put(s)
             clamp(s - 1)
-            if s in (1, 3):
+            if s < PACK and s % 2 == 1:
                 weave_pair(page_bf0, page_pair[s // 2], s - 1)
-            if s in (2, 4):
+            if s <= PACK and s % 2 == 0:
                 weave_pair(x_bf0, x_pair[s // 2 - 1], s - 2)
             if s >= PACK:
                 copy_lane(s - PACK)
@@ -301,25 +304,26 @@ def tile_list_launch_field_advisor_kernel(
         for i in range(2):
             cols = slice(i * PICK // 2, (i + 1) * PICK // 2)
             quantize(x_codes[0][:, cols], x_sc[0][:, cols], x_bf0[i])
-        fetch(5, "narrow0")
-        add(6, "narrow1")
-        clamp(5)
-        put(6)
-        weave_pair([x_bf1], x_pair[2], 0)
-        copy_lane(2)
+        last = SLICES - 1
+        fetch(last - 2, "narrow0")
+        add(last - 1, "narrow1")
+        clamp(last - 2)
+        put(last - 1)
+        weave_pair([x_bf1], x_pair[-1], 0)
+        copy_lane(PACK - 2)
         for i in range(2):
             cols = slice(i * T2 // 2, (i + 1) * T2 // 2)
             quantize(page_codes[0][:, cols], page_sc[0][:, cols], page_bf0[i])
-        fetch(6, "wide0")
-        add(7, "wide1")
-        clamp(6)
-        put(7)
+        fetch(last - 1, "wide0")
+        add(last, "wide1")
+        clamp(last - 1)
+        put(last)
         for mt in range(T2 // P):
             second_product(mt, 0)
-        copy_lane(3)
-        fetch(7)
+        copy_lane(PACK - 1)
+        fetch(last)
         quantize_chunk(0)
-        clamp(7)
+        clamp(last)
         quantize_chunk(1)
         quantize(x_codes[1][:], x_sc[1][:], x_bf1)
         for c in range(2, chunks):

import math
from contextlib import ExitStack

import concourse.mybir as mybir

F32 = mybir.dt.float32
BF16 = mybir.dt.bfloat16
I32 = mybir.dt.int32
U32 = mybir.dt.uint32
U16 = mybir.dt.uint16
U8 = mybir.dt.uint8
FP8X4 = mybir.dt.float8_e4m3fn_x4
FP4X4 = mybir.dt.float4_e2m1fn_x4
ALU = mybir.AluOpType
ACT = mybir.ActivationFunctionType

P = 128
PACK = 4
K = 1536
T = 2048
S = 512
H = 1024
T2 = 1024
PICK = 512
GROUP = P * PACK
GROUPS = H // GROUP
SLICES = GROUPS * PACK
FIRST_DIRECT = SLICES - 2

VECTOR_SQUARED = (1, 3, 5)
QUADRANTS = (0, 2, 1, 3)
FLOPS = 2 * K * H * S + 2 * H * T2 * PICK


def tile_list_launch_field_advisor_kernel(
    tc, tab_words, tab_scales, offs, w4_words, w4_scales, w1, frq, gain, page0, wgs, offs2, offs3, low, vec, slot, out
):
    nc = tc.nc
    with ExitStack() as ctx:
        lists = ctx.enter_context(tc.tile_pool(name="lists", bufs=1))
        keep = ctx.enter_context(tc.tile_pool(name="keep", bufs=1))
        psum = ctx.enter_context(tc.psum_pool(name="psum", bufs=1))

        list1 = lists.tile([P, S // 16], U16, name="list1")
        list2 = lists.tile([P, S // 16], U16, name="list2")
        list3 = lists.tile([P, PICK // 16], U16, name="list3")

        tab = [keep.tile([P, T], U32, name="tab%d" % a) for a in range(K // GROUP)]
        tab_sc = keep.tile([P, 2 * T], U8, name="tab_sc")
        w4_sc_raw = keep.tile([P, 2, H], U8, name="w4_sc_raw")
        w1_raw = [keep.tile([P, PACK, GROUP], F32, name="w1_raw%d" % b, tag="wide%d" % b, align_bytes=64) for b in range(GROUPS)]
        w4_raw = [keep.tile([P, 2, 2 * GROUP], U8, name="w4_raw%d" % b) for b in range(GROUPS)]
        page = [keep.tile([P, T2], F32, name="page%d" % s) for s in range(SLICES)]
        wg_first = keep.tile([P, S], F32, name="wg_first")
        wg_rest = keep.tile([P, PACK - 1, S], F32, name="wg_rest")
        frq_t = keep.tile([P, GROUPS, PACK], F32, name="frq_t")
        gain_t = keep.tile([P, GROUPS, PACK], F32, name="gain_t")
        low_t = keep.tile([P, GROUPS, PACK], F32, name="low_t")
        vec_t = keep.tile([P, GROUPS, PACK], F32, name="vec_t")

        def load_tab(a):
            nc.sync.dma_start(out=tab[a][:].bitcast(I32), in_=tab_words[a].rearrange("p t i -> p (t i)").bitcast(I32))

        def load_w1(b):
            nc.sync.dma_start(out=w1_raw[b][:], in_=w1[:, b * GROUP:(b + 1) * GROUP].rearrange("(p j) c -> p j c", j=PACK))

        def load_w4(b):
            nc.sync.dma_start(
                out=w4_raw[b][:].bitcast(I32),
                in_=w4_words[:, :, 2 * b * GROUP:2 * (b + 1) * GROUP].rearrange("a p c -> p a c").bitcast(I32),
            )

        def load_rows(queue, tile, vector):
            queue.dma_start(out=tile[:], in_=vector.rearrange("(b p t) -> p b t", p=P, t=PACK))

        def load_page(s):
            b, t = divmod(s, PACK)
            nc.sync.dma_start(out=page[s][:], in_=page0[b * GROUP:(b + 1) * GROUP, :].rearrange("(p t) m -> p t m", t=PACK)[:, t, :])

        nc.vector.memset(tab_sc[:].bitcast(I32), 0)
        nc.gpsimd.memset(w4_sc_raw[:].rearrange("p a c -> p (a c)").bitcast(I32), 0)

        nc.sync.dma_start(list1[:], offs)
        load_rows(nc.scalar, frq_t, frq)
        load_rows(nc.scalar, gain_t, gain)
        load_tab(1)
        for q in QUADRANTS:
            nc.scalar.dma_start(out=tab_sc[32 * q:32 * q + 4, T:2 * T].bitcast(I32), in_=tab_scales[1, 4 * q:4 * q + 4, :].bitcast(I32))
        load_w1(0)
        for q in QUADRANTS:
            nc.sync.dma_start(
                out=w4_sc_raw[32 * q:32 * q + 4, :, :].bitcast(I32),
                in_=w4_scales[:, 4 * q:4 * q + 4, :].rearrange("a r c -> r a c").bitcast(I32),
            )
        load_w4(0)
        load_tab(0)
        for q in QUADRANTS:
            nc.sync.dma_start(out=tab_sc[32 * q:32 * q + 8, 0:T].bitcast(I32), in_=tab_scales[0:3:2, 4 * q:4 * q + 4, :].bitcast(I32))
        nc.sync.dma_start(list2[:], offs2)
        load_tab(2)
        load_page(0)
        wgs_rows = wgs.rearrange("(p t) j -> p t j", t=PACK)
        for q in QUADRANTS:
            nc.sync.dma_start(out=wg_first[32 * q:32 * (q + 1), :], in_=wgs_rows[:, 0, :])
        for q in QUADRANTS:
            nc.sync.dma_start(out=wg_rest[32 * q:32 * (q + 1), :, :], in_=wgs_rows[:, 1:PACK, :])
        load_page(1)
        nc.sync.dma_start(list3[:], offs3)
        load_w1(1)
        load_rows(nc.sync, low_t, low)
        load_rows(nc.sync, vec_t, vec)
        load_w4(1)
        for s in range(2, SLICES):
            load_page(s)

        half_frq = keep.tile([P, GROUPS, PACK], F32, name="half_frq")
        gain_m2 = keep.tile([P, GROUPS, PACK], F32, name="gain_m2")
        shift = keep.tile([P, 1], F32, name="shift")
        nc.vector.memset(shift[:], 1.0)
        nc.scalar.activation(out=shift[:], in_=shift[:], func=ACT.Copy, scale=-math.pi / 4)
        nc.scalar.activation(out=half_frq[:], in_=frq_t[:], func=ACT.Copy, scale=0.5)
        nc.scalar.activation(out=gain_m2[:], in_=gain_t[:], func=ACT.Copy, scale=-2.0)

        picked = [keep.tile([P, S], U32, name="picked%d" % a, align_bytes=64) for a in range(K // GROUP)]
        picked_sc = [keep.tile([P, S], U8, name="picked_sc%d" % w, align_bytes=64) for w in range(2)]
        nc.vector.tensor_copy(picked[1][:], tab[1][:].indirect(list1[:]))
        nc.vector.tensor_copy(picked_sc[1][:], tab_sc[:, T:2 * T].indirect(list1[:]))

        w1_codes = [keep.tile([P, GROUP], U32, name="w1_codes%d" % b, align_bytes=64) for b in range(GROUPS)]
        w1_sc = [keep.tile([P, GROUP], U8, name="w1_sc%d" % b, align_bytes=64) for b in range(GROUPS)]
        w4_codes = [keep.tile([P, 2, 2 * GROUP], U8, name="w4_codes%d" % b, align_bytes=64) for b in range(GROUPS)]
        w4_sc = [keep.tile([P, 2, GROUP], U8, name="w4_sc%d" % b, align_bytes=64) for b in range(GROUPS)]

        def prepare_weights(b):
            w1_bf = keep.tile([P, GROUP * PACK], BF16, name="w1_bf", align_bytes=64)
            nc.scalar.copy(
                out=w1_bf[:].rearrange("p (t q j) -> p q j t", t=PACK, j=PACK),
                in_=w1_raw[b][:].rearrange("p j (q t) -> p q j t", t=PACK),
            )
            nc.scalar.copy(
                out=w4_codes[b][:].bitcast(U16).rearrange("p a (t q) -> p a t q", t=PACK),
                in_=w4_raw[b][:].bitcast(U16).rearrange("p a (q t) -> p a t q", t=PACK),
            )
            nc.vector.quantize_mx(out=w1_codes[b][:].bitcast(FP8X4), scales=w1_sc[b][:], in_=w1_bf[:])

        def deal_w4_scales(b):
            nc.vector.tensor_copy(
                out=w4_sc[b][:].rearrange("p a (t q) -> p a t q", t=PACK),
                in_=w4_sc_raw[:, :, b * GROUP:(b + 1) * GROUP].rearrange("p a (q t) -> p a t q", t=PACK),
            )

        deal_w4_scales(0)
        prepare_weights(0)
        nc.vector.tensor_copy(picked[0][:], tab[0][:].indirect(list1[:]))
        nc.vector.tensor_copy(picked_sc[0][:], tab_sc[:, 0:T].indirect(list1[:]))
        half = S // 2
        for c0 in (0, half):
            nc.vector.tensor_copy(picked[2][:, c0:c0 + half], tab[2][:].indirect(list1[:, c0 // 16:(c0 + half) // 16]))
        deal_w4_scales(1)

        y = {}
        wave = {}

        def first_product(s, c0, c1, bank):
            b, t = divmod(s, PACK)
            acc = psum.tile([P, c1 - c0], F32, name="y%d_%d" % (s, c0), tag="bank%d" % bank)
            for a in (1, 0):
                nc.tensor.matmul_mx(
                    out=acc[:],
                    lhsT=w4_codes[b][:, a, 2 * P * t:2 * P * (t + 1)].bitcast(FP4X4),
                    lhsT_scale=w4_sc[b][:, a, P * t:P * (t + 1)],
                    rhs=picked[a][:, c0:c1].bitcast(FP8X4),
                    rhs_scale=picked_sc[a][:, c0:c1],
                    start=(a == 1),
                    stop=False,
                )
            nc.tensor.matmul_mx(
                out=acc[:],
                lhsT=w1_codes[b][:, P * t:P * (t + 1)].bitcast(FP8X4),
                lhsT_scale=w1_sc[b][:, P * t:P * (t + 1)],
                rhs=picked[2][:, c0:c1].bitcast(FP8X4),
                rhs_scale=picked_sc[0][4:P, c0:c1],
                start=False,
                stop=True,
            )
            y[s, c0] = acc

        def sine(s, parts):
            b, t = divmod(s, PACK)
            z = wave[s] = keep.tile([P, S], F32, name="wave%d" % s, tag="wave%d" % s)
            squared = keep.tile([P, S], F32, name="sq%d" % s, tag="stage%d" % s)
            for c0, c1 in parts:
                nc.scalar.activation(out=z[:, c0:c1], in_=y[s, c0][:], func=ACT.Sin, bias=shift[:], scale=half_frq[:, b, t:t + 1])
            for c0, c1 in parts:
                nc.scalar.activation(out=squared[:, c0:c1], in_=z[:, c0:c1], func=ACT.Square)
            for c0, c1 in parts:
                nc.scalar.activation(
                    out=z[:, c0:c1], in_=squared[:, c0:c1], func=ACT.Identity, bias=gain_t[:, b, t:t + 1], scale=gain_m2[:, b, t:t + 1]
                )
            return squared

        halves = ((0, half), (half, S))
        whole = ((0, S),)
        first_product(0, 0, half, 0)
        first_product(0, half, S, SLICES - 1)
        sine(0, halves)
        for c0, c1 in halves:
            nc.vector.tensor_tensor(out=wave[0][:, c0:c1], in0=y[0, c0][:], in1=wave[0][:, c0:c1], op=ALU.add)
        for s in range(1, SLICES):
            first_product(s, 0, S, s)
            last_squared = sine(s, whole)
            if s == 1:
                prepare_weights(1)

        warm = keep.tile([P, 1], F32, name="warm")
        nc.scalar.activation(out=warm[:], in_=last_squared[:, 0:1], func=ACT.Abs_reciprocal_sqrt, bias=shift[:], scale=-1.0)

        chunk = 2 * P
        chunks = T2 // chunk
        x_pair = [keep.tile([P, 2, PICK], F32, name="x_pair%d" % i, tag="x_pair%d" % i) for i in range(FIRST_DIRECT // 2)]
        page_pair = [keep.tile([P, 2, T2], F32, name="page_pair%d" % i) for i in range(2)]
        x_bf0 = [keep.tile([P, PICK // 2, PACK], BF16, name="x_bf0_%d" % i, tag="narrow%d" % i, align_bytes=64) for i in range(2)]
        x_bf1 = keep.tile([P, PICK, PACK], BF16, name="x_bf1", align_bytes=64)
        page_bf0 = [keep.tile([P, T2 // 2, PACK], BF16, name="page_bf0_%d" % i, tag="wide%d" % i, align_bytes=64) for i in range(2)]
        page_bf1 = [keep.tile([P, chunk, PACK], BF16, name="page_bf1_%d" % c, align_bytes=64) for c in range(chunks)]
        x_codes = [keep.tile([P, PICK], U32, name="x_codes%d" % b, align_bytes=64) for b in range(GROUPS)]
        x_sc = [keep.tile([P, PICK], U8, name="x_sc%d" % b, align_bytes=64) for b in range(GROUPS)]
        page_codes = [keep.tile([P, T2], U32, name="page_codes%d" % b, align_bytes=64) for b in range(GROUPS)]
        page_sc = [keep.tile([P, T2], U8, name="page_sc%d" % b, align_bytes=64) for b in range(GROUPS)]

        def weave_pair(tiles, pair, t0):
            width = pair.shape[2] // len(tiles)
            for n, dst in enumerate(tiles):
                nc.scalar.copy(out=dst[:, :, t0:t0 + 2], in_=pair[:, :, n * width:(n + 1) * width].rearrange("p t c -> p c t"))

        h = {}
        fetched = {}

        def add(s, tag=None):
            h[s] = wave[s] if tag is None else keep.tile([P, S], F32, name="h%d" % s, tag=tag, align_bytes=64)
            nc.vector.tensor_tensor(out=h[s][:], in0=y[s, 0][:], in1=wave[s][:], op=ALU.add)

        def put(s):
            b, t = divmod(s, PACK)
            nc.vector.tensor_tensor(page[s][:].indirect(list2[:]), h[s][:], wg_first[:] if t == 0 else wg_rest[:, t - 1, :], ALU.mult)
            if b == 0:
                nc.sync.dma_start(out=page_pair[t // 2][:, t % 2, :], in_=page[s][:])

        def fetch(s, tag=None):
            if tag is None:
                fetched[s] = keep.tile([P, PICK], F32, name="fetched%d" % s, tag="stage%d" % ((s + 1) % SLICES))
            else:
                fetched[s] = keep.tile([P, PICK], F32, name="fetched%d" % s, tag=tag, align_bytes=64)
            nc.vector.tensor_copy(fetched[s][:], page[s][:].indirect(list3[:]))

        def clamp(s):
            b, t = divmod(s, PACK)
            dst = x_pair[s // 2][:, s % 2, :] if s < FIRST_DIRECT else x_bf1[:, :, t]
            nc.vector.tensor_scalar(dst, fetched[s][:], low_t[:, b, t:t + 1], vec_t[:, b, t:t + 1], ALU.max, ALU.mult)

        def quantize(codes, scales, values):
            nc.vector.quantize_mx(out=codes.bitcast(FP8X4), scales=scales, in_=values[:].rearrange("p c t -> p (c t)"))

        def quantize_chunk(c):
            cols = slice(c * chunk, (c + 1) * chunk)
            quantize(page_codes[1][:, cols], page_sc[1][:, cols], page_bf1[c])

        def copy_lane(t):
            for c in range(chunks):
                nc.scalar.copy(out=page_bf1[c][:, :, t], in_=page[PACK + t][:, c * chunk:(c + 1) * chunk])

        scores = []

        def second_product(mt, b):
            if b == 0:
                scores.append(psum.tile([P, PICK], F32, name="e%d" % mt, tag="bank%d" % mt))
            nc.tensor.matmul_mx(
                out=scores[mt][:],
                lhsT=page_codes[b][:, P * mt:P * (mt + 1)].bitcast(FP8X4),
                lhsT_scale=page_sc[b][:, P * mt:P * (mt + 1)],
                rhs=x_codes[b][:].bitcast(FP8X4),
                rhs_scale=x_sc[b][:],
                start=(b == 0),
                stop=(b == GROUPS - 1),
            )

        for c0, c1 in halves:
            nc.vector.tensor_tensor(page[0][:].indirect(list2[:, c0 // 16:c1 // 16]), wave[0][:, c0:c1], wg_first[:, c0:c1], ALU.mult)
        nc.sync.dma_start(out=page_pair[0][:, 0, :], in_=page[0][:])
        for s in range(1, FIRST_DIRECT):
            add(s)
            fetch(s - 1)
            put(s)
            clamp(s - 1)
            if s < PACK and s % 2 == 1:
                weave_pair(page_bf0, page_pair[s // 2], s - 1)
            if s <= PACK and s % 2 == 0:
                weave_pair(x_bf0, x_pair[s // 2 - 1], s - 2)
            if s >= PACK:
                copy_lane(s - PACK)
        slot_t = keep.tile([P, T2 // P], F32, name="slot_t", tag="x_pair0")
        with nc.allow_non_contiguous_dma(reason="one slot value for each output row"):
            nc.sync.dma_start(out=slot_t[:], in_=slot.rearrange("(c p) -> p c", p=P))
        for i in range(2):
            cols = slice(i * PICK // 2, (i + 1) * PICK // 2)
            quantize(x_codes[0][:, cols], x_sc[0][:, cols], x_bf0[i])
        last = SLICES - 1
        fetch(last - 2, "narrow0")
        add(last - 1, "narrow1")
        clamp(last - 2)
        put(last - 1)
        weave_pair([x_bf1], x_pair[-1], 0)
        copy_lane(PACK - 2)
        for i in range(2):
            cols = slice(i * T2 // 2, (i + 1) * T2 // 2)
            quantize(page_codes[0][:, cols], page_sc[0][:, cols], page_bf0[i])
        fetch(last - 1, "wide0")
        add(last, "wide1")
        clamp(last - 1)
        put(last)
        for mt in range(T2 // P):
            second_product(mt, 0)
        copy_lane(PACK - 1)
        fetch(last)
        quantize_chunk(0)
        clamp(last)
        quantize_chunk(1)
        quantize(x_codes[1][:], x_sc[1][:], x_bf1)
        for c in range(2, chunks):
            quantize_chunk(c)

        for mt in range(T2 // P):
            second_product(mt, 1)
            root = keep.tile([P, PICK], F32, name="root%d" % mt, tag="wave%d" % mt)
            result = keep.tile([P, PICK], F32, name="result%d" % mt, tag="stage%d" % mt)
            if mt in VECTOR_SQUARED:
                nc.vector.tensor_copy(out=result[:], in_=scores[mt][:])
                nc.vector.tensor_tensor(out=root[:], in0=scores[mt][:], in1=result[:], op=ALU.mult)
            else:
                nc.scalar.activation(out=root[:], in_=scores[mt][:], func=ACT.Square)
            nc.scalar.activation(out=root[:], in_=root[:], func=ACT.Abs_reciprocal_sqrt, bias=slot_t[:, mt:mt + 1])
            nc.vector.tensor_tensor(out=result[:], in0=root[:], in1=root[:], op=ALU.mult)
            nc.sync.dma_start(out=out[P * mt:P * (mt + 1), :], in_=result[:])
